import numpy as np, ml_dtypes
CORES = [4,12,20,132,140,148,260,268,276,388,396,404]
N = 12
G1 = [0,1,2,3,4,5,6,7,8,9,10,11]
ROOT1 = 2
G2 = [3,4,5,6,7,8,9,10,11]
G3 = [0,1,2]
def setup_inputs(rng):
    return {"x1": rng.standard_normal((N, 128, 16), dtype=np.float32), "x2": rng.standard_normal((N, 128, 512), dtype=np.float32), "x3": rng.standard_normal((N, 128, 8), dtype=np.float32).astype(ml_dtypes.bfloat16)}
def reference(x1, x2, x3):
    out = {}
    y = np.full((N, 128, 16), np.nan, x1.dtype)
    for r in G1:
        y[r] = x1[G1[ROOT1]]
    out["y1"] = y
    y = np.full((N, 128, 512), np.nan, x2.dtype)
    s = x2[G2].sum(axis=0, dtype=np.float64).astype(x2.dtype)
    for r in G2:
        y[r] = s
    out["y2"] = y
    y = np.full((N, 128, 8), np.nan, x3.dtype)
    for i, r in enumerate(G3):
        y[G3[(i + 1) % 3]] = x3[r]
    out["y3"] = y
    return out

@@ -1,0 +1,220 @@
+from concourse.bass import DstId, RemoteDMATransfer
+
+WORLD = 512
+NSLAB = 4
+NCALL = 2
+ROWS = 128 // NSLAB
+
+SCRATCH = {
+    "a": ("dram", [NSLAB, 128, 128], "float32"),
+    "b": ("dram", [NSLAB, 128, 128], "float32"),
+    "c1": ("dram", [128, 16], "float32"),
+    "s3": ("dram", [128, 8], "bfloat16"),
+    "l3": ("dram", [128, 8], "bfloat16"),
+}
+SEMAPHORES = (["sent", "s1", "s2", "b1", "b3", "ldb", "ld3", "gst", "sty", "st3", "stq0", "stq1"]
+              + ["ld%d" % p for p in range(NCALL)] + ["fin%d" % p for p in range(NCALL)])
+
+_PLAN = {}
+
+
+def _n(mask):
+    return bin(mask).count("1")
+
+
+def _split(mask, n):
+    bits = [i for i in range(mask.bit_length()) if (mask >> i) & 1]
+    w = len(bits) // n
+    return [sum(1 << e for e in bits[i * w:(i + 1) * w]) for i in range(n)]
+
+
+def _common(topo, src, dsts):
+    m = topo.mask(src, dsts[0])
+    for d in dsts[1:]:
+        m &= topo.mask(src, d)
+    return m
+
+
+def _plan(T, topo):
+    if "p" in _PLAN:
+        return _PLAN["p"]
+    cores = list(T.cores)
+    tb = T.tables
+    world = range(WORLD)
+
+    def chip_cores(c):
+        return [d for d in world if topo.host(d) == topo.host(c) and topo.chip(d) == topo.chip(c)]
+
+    def port_cores(c):
+        mate = [d for d in world if topo.mates(c, d)][0]
+        own = [d for d in chip_cores(c) if d not in cores and topo.may_write(d, mate)]
+        dies = sorted({topo.die(d) for d in own}, key=lambda x: x != topo.die(c))
+        by = [[d for d in own if topo.die(d) == x] for x in dies]
+        return [by[i % len(by)][i // len(by)] for i in range(len(own))]
+
+    P = {}
+    mem = [cores[r] for r in tb["G2"]]
+    hosts = sorted({topo.host(c) for c in mem})
+    col = {}
+    for c in mem:
+        col.setdefault(topo.chip(c), []).append(c)
+    for k in col:
+        col[k].sort(key=topo.host)
+    hub = [h for h in hosts
+           if all(topo.may_write(c, d) and topo.may_write(d, c)
+                  for k in col for c in col[k] for d in col[k] if topo.host(d) == h and c != d)][0]
+    red = {}
+    for k in col:
+        hubrank = [c for c in col[k] if topo.host(c) == hub][0]
+        red[k] = port_cores(hubrank)[:NSLAB]
+    P["mem"], P["col"], P["red"] = mem, col, red
+    P["role"] = {red[k][m]: (k, m) for k in red for m in range(NSLAB)}
+    busy = set(cores) | set(P["role"])
+
+    g1 = [cores[r] for r in tb["G1"]]
+    root = g1[tb["ROOT1"]]
+    dests = [d for d in g1 if d != root]
+    direct = [d for d in dests if topo.may_write(root, d)]
+    rest = [d for d in dests if d not in direct]
+    relays = {}
+    for rk in sorted({topo.rack(topo.host(d)) for d in rest}):
+        ds = [d for d in rest if topo.rack(topo.host(d)) == rk]
+        cands = [c for c in world if c not in busy and topo.rack(topo.host(c)) == rk and topo.chip(c) == topo.chip(root)
+                 and topo.may_write(root, c) and all(topo.may_write(c, d) for d in ds)]
+        cands.sort(key=lambda c: (topo.host(c) != topo.host(root), topo.die(c) != topo.die(root)))
+        relays[cands[0]] = ds
+        busy.add(cands[0])
+    P["root"], P["direct"], P["relays"], P["g1"] = root, direct, relays, g1
+    from1 = {d: root for d in direct + list(relays)}
+    for c in relays:
+        for d in relays[c]:
+            from1[d] = c
+    P["mask1"] = {root: _common(topo, root, direct + list(relays))}
+    for c in relays:
+        P["mask1"][c] = _common(topo, c, relays[c])
+    P["from1"] = from1
+
+    g3 = [cores[r] for r in tb["G3"]]
+    nxt, prev = {}, {}
+    for i, s in enumerate(g3):
+        d = g3[(i + 1) % len(g3)]
+        if topo.may_write(s, d):
+            nxt[s], prev[d] = d, s
+        else:
+            rl = [c for c in port_cores(s) if c not in busy and topo.may_write(c, d)][0]
+            busy.add(rl)
+            nxt[s], prev[rl], nxt[rl], prev[d] = rl, s, d, rl
+    P["g3"], P["nxt"], P["prev"] = g3, nxt, prev
+    _PLAN["p"] = P
+    return P
+
+
+def rank_program(g, core, T, topo):
+    P = _plan(T, topo)
+    sem = T.sem
+    sent = [0]
+
+    def dst(d):
+        rid, pid = topo.addr(d, core)
+        return DstId(rid=rid, pnc=pid)
+
+    def call(specs):
+        trs = []
+        for mask, rsem, srcs, outs in specs:
+            trs.append(RemoteDMATransfer(dst_ids=[dst(d) for d, _ in outs], dma_engine_mask=mask, remote_sem=rsem,
+                                         srcs=list(srcs), dsts=[ap for _, ap in outs], alu_op=1 if len(srcs) > 1 else 0))
+            sent[0] += _n(mask)
+        g.remote_dma_fused(trs, local_sem=sem.sent)
+
+    mem, col, red = P["mem"], P["col"], P["red"]
+    per = NSLAB // NCALL
+    queues = (g.sync, g.scalar)
+    in2 = core in mem
+    in3 = core in P["g3"]
+    in1 = core in P["g1"]
+    root = P["root"]
+
+    if in2:
+        for p in range(NCALL):
+            queues[p % 2].dma_start(T.a[p * per:(p + 1) * per], T.x2[p * per * ROWS:(p + 1) * per * ROWS, :]).then_inc(
+                sem["ld%d" % p], 16)
+    if core == root:
+        g.sync.dma_start(T.c1[:], T.x1[:]).then_inc(sem.ldb, 16)
+        g.scalar.dma_start(T.y1[:], T.x1[:]).then_inc(sem.sty, 16)
+    if in3:
+        g.sync.dma_start(T.s3[:], T.x3[:]).then_inc(sem.ld3, 16)
+
+    if in2:
+        k = topo.chip(core)
+        hi = col[k].index(core)
+        for p in range(NCALL):
+            slabs = list(range(p * per, (p + 1) * per))
+            masks = _split(_common(topo, core, [red[k][m] for m in slabs]), per)
+            g.wait_ge(sem["ld%d" % p], 16)
+            call([(mk, sem.s1, [T.a[m]], [(red[k][m], T.a[hi])]) for m, mk in zip(slabs, masks)])
+
+    if core in P["role"]:
+        k, m = P["role"][core]
+        p = m // per
+        nh = len(col[k])
+        others = [x for x in sorted(col) if x != k]
+        arrive = 0
+        for c in col[k]:
+            slabs = list(range(p * per, (p + 1) * per))
+            arrive += _n(_split(_common(topo, c, [red[k][x] for x in slabs]), per)[m - p * per])
+        raw = [T.a[i] for i in range(nh)]
+        peers = [red[x][m] for x in others]
+        g.wait_ge(sem.s1, arrive)
+        call([(_common(topo, core, peers), sem.s2, raw,
+               [(red[x][m], T.b[[y for y in sorted(col) if y != x].index(k)]) for x in others])])
+        g.wait_ge(sem.s2, sum(_n(_common(topo, red[x][m], [red[y][m] for y in sorted(col) if y != x])) for x in others))
+        call([(_common(topo, core, col[k]), sem["fin%d" % p], raw + [T.b[i] for i in range(len(others))],
+               [(c, T.b[m]) for c in col[k]])])
+
+    if core == root:
+        g.wait_ge(sem.ldb, 16)
+        call([(P["mask1"][root], sem.b1, [T.c1[:]], [(d, T.c1[:]) for d in P["direct"] + list(P["relays"])])])
+    if core in P["relays"]:
+        g.wait_ge(sem.b1, _n(P["mask1"][root]))
+        call([(P["mask1"][core], sem.b1, [T.c1[:]], [(d, T.c1[:]) for d in P["relays"][core]])])
+
+    if core in P["nxt"]:
+        d = P["nxt"][core]
+        if in3:
+            g.wait_ge(sem.ld3, 16)
+            src = T.s3[:]
+        else:
+            g.wait_ge(sem.b3, _n(topo.mask(P["prev"][core], core)))
+            src = T.l3[:]
+        call([(topo.mask(core, d), sem.b3, [src], [(d, T.l3[:])])])
+
+    if in2:
+        k = topo.chip(core)
+        used = [0, 0]
+        for p in range(NCALL):
+            q = queues[p % 2]
+            q.wait_ge(sem["fin%d" % p], sum(_n(_common(topo, red[k][m], col[k])) for m in range(p * per, (p + 1) * per)))
+            q.dma_start(T.y2[p * per * ROWS:(p + 1) * per * ROWS, :], T.b[p * per:(p + 1) * per]).then_inc(
+                sem["stq%d" % (p % 2)], 16)
+            used[p % 2] += 16
+        for i in range(2):
+            if used[i]:
+                queues[i].wait_ge(sem["stq%d" % i], used[i])
+    if in3:
+        g.sync.wait_ge(sem.b3, _n(topo.mask(P["prev"][core], core)))
+        g.sync.dma_start(T.y3[:], T.l3[:]).then_inc(sem.st3, 16)
+        g.sync.wait_ge(sem.st3, 16)
+    if core == root:
+        g.scalar.wait_ge(sem.sty, 16)
+    elif in1:
+        n1 = _n(P["mask1"][P["from1"][core]])
+        if in2:
+            g.wait_ge(sem.b1, n1)
+            g.dma_start(T.y1[:], T.c1[:]).then_inc(sem.gst, 16)
+            g.wait_ge(sem.gst, 16)
+        else:
+            g.scalar.wait_ge(sem.b1, n1)
+            g.scalar.dma_start(T.y1[:], T.c1[:]).then_inc(sem.sty, 16)
+            g.scalar.wait_ge(sem.sty, 16)
+    if sent[0]:
+        g.wait_ge(sem.sent, sent[0])

@@ -2,7 +2,7 @@ from concourse.bass import DstId, RemoteDMATransfer
 
 WORLD = 512
 NSLAB = 4
-NCALL = 2
+NCALL = 4
 ROWS = 128 // NSLAB
 
 SCRATCH = {
@@ -12,7 +12,7 @@ SCRATCH = {
     "s3": ("dram", [128, 8], "bfloat16"),
     "l3": ("dram", [128, 8], "bfloat16"),
 }
-SEMAPHORES = (["sent", "s1", "s2", "b1", "b3", "ldb", "ld3", "gst", "sty", "st3", "stq0", "stq1"]
+SEMAPHORES = (["sent", "s1", "s2", "b1", "b3", "ldb", "ldx", "gst", "sty", "st3", "stq0", "stq1"]
               + ["ld%d" % p for p in range(NCALL)] + ["fin%d" % p for p in range(NCALL)])
 
 _PLAN = {}
@@ -142,7 +142,7 @@ def rank_program(g, core, T, topo):
         g.sync.dma_start(T.c1[:], T.x1[:]).then_inc(sem.ldb, 16)
         g.scalar.dma_start(T.y1[:], T.x1[:]).then_inc(sem.sty, 16)
     if in3:
-        g.sync.dma_start(T.s3[:], T.x3[:]).then_inc(sem.ld3, 16)
+        g.sync.dma_start(T.s3[:], T.x3[:]).then_inc(sem.ldx, 16)
 
     if in2:
         k = topo.chip(core)
@@ -181,7 +181,7 @@ def rank_program(g, core, T, topo):
     if core in P["nxt"]:
         d = P["nxt"][core]
         if in3:
-            g.wait_ge(sem.ld3, 16)
+            g.wait_ge(sem.ldx, 16)
             src = T.s3[:]
         else:
             g.wait_ge(sem.b3, _n(topo.mask(P["prev"][core], core)))

@@ -2,7 +2,7 @@ from concourse.bass import DstId, RemoteDMATransfer
 
 WORLD = 512
 NSLAB = 4
-NCALL = 4
+NST = 2
 ROWS = 128 // NSLAB
 
 SCRATCH = {
@@ -12,8 +12,8 @@ SCRATCH = {
     "s3": ("dram", [128, 8], "bfloat16"),
     "l3": ("dram", [128, 8], "bfloat16"),
 }
-SEMAPHORES = (["sent", "s1", "s2", "b1", "b3", "ldb", "ldx", "gst", "sty", "st3", "stq0", "stq1"]
-              + ["ld%d" % p for p in range(NCALL)] + ["fin%d" % p for p in range(NCALL)])
+SEMAPHORES = (["sent", "s0", "s1", "s2", "b1", "b3", "ldb", "ldx", "gst", "sty", "st3", "stq0", "stq1", "lda", "ldd"]
+              + ["fin%d" % p for p in range(NST)])
 
 _PLAN = {}
 
@@ -45,12 +45,28 @@ def _plan(T, topo):
     def chip_cores(c):
         return [d for d in world if topo.host(d) == topo.host(c) and topo.chip(d) == topo.chip(c)]
 
+    def owns_port(d):
+        return topo.may_write(d, [e for e in world if topo.mates(d, e)][0])
+
     def port_cores(c):
-        mate = [d for d in world if topo.mates(c, d)][0]
-        own = [d for d in chip_cores(c) if d not in cores and topo.may_write(d, mate)]
-        dies = sorted({topo.die(d) for d in own}, key=lambda x: x != topo.die(c))
+        own = [d for d in chip_cores(c) if d not in cores and owns_port(d)]
+        dies = sorted({topo.die(d) for d in own}, key=lambda x: x == topo.die(c))
         by = [[d for d in own if topo.die(d) == x] for x in dies]
         return [by[i % len(by)][i // len(by)] for i in range(len(own))]
+
+    def lanes(c, with_rank, reds):
+        out = [None] * len(reds)
+        for die in sorted({topo.die(r) for r in reds}):
+            slabs = [m for m in range(len(reds)) if topo.die(reds[m]) == die]
+            pick = []
+            for port in (True, False):
+                cl = [d for d in chip_cores(c) if topo.die(d) == die and owns_port(d) == port]
+                if c in cl:
+                    cl = [c] if with_rank else [d for d in cl if d != c]
+                pick.append(cl[0])
+            for m, d in zip(slabs, pick if with_rank else pick[::-1]):
+                out[m] = d
+        return out
 
     P = {}
     mem = [cores[r] for r in tb["G2"]]
@@ -63,13 +79,18 @@ def _plan(T, topo):
     hub = [h for h in hosts
            if all(topo.may_write(c, d) and topo.may_write(d, c)
                   for k in col for c in col[k] for d in col[k] if topo.host(d) == h and c != d)][0]
-    red = {}
+    red, fin, snd = {}, {}, {}
     for k in col:
         hubrank = [c for c in col[k] if topo.host(c) == hub][0]
         red[k] = port_cores(hubrank)[:NSLAB]
-    P["mem"], P["col"], P["red"] = mem, col, red
-    P["role"] = {red[k][m]: (k, m) for k in red for m in range(NSLAB)}
-    busy = set(cores) | set(P["role"])
+        fin[k] = lanes(hubrank, False, red[k])
+        for c in col[k]:
+            snd[c] = [c] * NSLAB if c == hubrank else lanes(c, True, red[k])
+    P["mem"], P["col"], P["red"], P["fin"], P["snd"] = mem, col, red, fin, snd
+    P["redrole"] = {red[k][m]: (k, m) for k in red for m in range(NSLAB)}
+    P["finrole"] = {fin[k][m]: (k, m) for k in fin for m in range(NSLAB)}
+    P["fwdrole"] = {snd[c][m]: (c, m) for c in snd for m in range(NSLAB) if snd[c][m] != c}
+    busy = set(cores) | set(P["redrole"]) | set(P["finrole"]) | set(P["fwdrole"])
 
     g1 = [cores[r] for r in tb["G1"]]
     root = g1[tb["ROOT1"]]
@@ -109,6 +130,22 @@ def _plan(T, topo):
     return P
 
 
+def _hop1_masks(topo, P, c):
+    k = topo.chip(c)
+    snd, red = P["snd"][c], P["red"][k]
+    fw = [m for m in range(NSLAB) if snd[m] != c]
+    own = [m for m in range(NSLAB) if snd[m] == c]
+    out = {}
+    if fw:
+        parts = _split(_common(topo, c, [snd[m] for m in fw]), NSLAB)[::-1]
+        for i, m in enumerate(fw):
+            out[m] = (parts[i], topo.mask(snd[m], red[m]))
+    parts = _split(_common(topo, c, [red[m] for m in own]), len(own))
+    for i, m in enumerate(own):
+        out[m] = (None, parts[i])
+    return fw, own, out
+
+
 def rank_program(g, core, T, topo):
     P = _plan(T, topo)
     sem = T.sem
@@ -126,18 +163,22 @@ def rank_program(g, core, T, topo):
             sent[0] += _n(mask)
         g.remote_dma_fused(trs, local_sem=sem.sent)
 
-    mem, col, red = P["mem"], P["col"], P["red"]
-    per = NSLAB // NCALL
+    mem, col, red, fin, snd = P["mem"], P["col"], P["red"], P["fin"], P["snd"]
+    chips = sorted(col)
     queues = (g.sync, g.scalar)
     in2 = core in mem
     in3 = core in P["g3"]
     in1 = core in P["g1"]
     root = P["root"]
 
+    def x2rows(lo, hi):
+        return T.x2[lo * ROWS:hi * ROWS, :]
+
     if in2:
-        for p in range(NCALL):
-            queues[p % 2].dma_start(T.a[p * per:(p + 1) * per], T.x2[p * per * ROWS:(p + 1) * per * ROWS, :]).then_inc(
-                sem["ld%d" % p], 16)
+        fw, own, masks = _hop1_masks(topo, P, core)
+        if fw:
+            g.sync.dma_start(T.a[fw[0]:fw[-1] + 1], x2rows(fw[0], fw[-1] + 1)).then_inc(sem.lda, 16)
+        g.scalar.dma_start(T.a[own[0]:own[-1] + 1], x2rows(own[0], own[-1] + 1)).then_inc(sem.ldd, 16)
     if core == root:
         g.sync.dma_start(T.c1[:], T.x1[:]).then_inc(sem.ldb, 16)
         g.scalar.dma_start(T.y1[:], T.x1[:]).then_inc(sem.sty, 16)
@@ -147,28 +188,34 @@ def rank_program(g, core, T, topo):
     if in2:
         k = topo.chip(core)
         hi = col[k].index(core)
-        for p in range(NCALL):
-            slabs = list(range(p * per, (p + 1) * per))
-            masks = _split(_common(topo, core, [red[k][m] for m in slabs]), per)
-            g.wait_ge(sem["ld%d" % p], 16)
-            call([(mk, sem.s1, [T.a[m]], [(red[k][m], T.a[hi])]) for m, mk in zip(slabs, masks)])
+        if fw:
+            g.wait_ge(sem.lda, 16)
+            call([(masks[m][0], sem.s0, [T.a[m]], [(snd[core][m], T.a[m])]) for m in fw])
+        g.wait_ge(sem.ldd, 16)
+        call([(masks[m][1], sem.s1, [T.a[m]], [(red[k][m], T.a[hi])]) for m in own])
 
-    if core in P["role"]:
-        k, m = P["role"][core]
-        p = m // per
-        nh = len(col[k])
-        others = [x for x in sorted(col) if x != k]
-        arrive = 0
-        for c in col[k]:
-            slabs = list(range(p * per, (p + 1) * per))
-            arrive += _n(_split(_common(topo, c, [red[k][x] for x in slabs]), per)[m - p * per])
-        raw = [T.a[i] for i in range(nh)]
-        peers = [red[x][m] for x in others]
-        g.wait_ge(sem.s1, arrive)
-        call([(_common(topo, core, peers), sem.s2, raw,
-               [(red[x][m], T.b[[y for y in sorted(col) if y != x].index(k)]) for x in others])])
-        g.wait_ge(sem.s2, sum(_n(_common(topo, red[x][m], [red[y][m] for y in sorted(col) if y != x])) for x in others))
-        call([(_common(topo, core, col[k]), sem["fin%d" % p], raw + [T.b[i] for i in range(len(others))],
+    if core in P["fwdrole"]:
+        c, m = P["fwdrole"][core]
+        k = topo.chip(c)
+        mk = _hop1_masks(topo, P, c)[2][m]
+        g.wait_ge(sem.s0, _n(mk[0]))
+        call([(mk[1], sem.s1, [T.a[m]], [(red[k][m], T.a[col[k].index(c)])])])
+
+    def mask2(x, m):
+        return _common(topo, red[x][m], [fin[y][m] for y in chips])
+
+    if core in P["redrole"]:
+        k, m = P["redrole"][core]
+        g.wait_ge(sem.s1, sum(_n(_hop1_masks(topo, P, c)[2][m][1]) for c in col[k]))
+        call([(mask2(k, m), sem.s2, [T.a[i] for i in range(len(col[k]))], [(fin[y][m], T.b[chips.index(k)]) for y in chips])])
+
+    def mask3(k, m):
+        return _common(topo, fin[k][m], col[k])
+
+    if core in P["finrole"]:
+        k, m = P["finrole"][core]
+        g.wait_ge(sem.s2, sum(_n(mask2(x, m)) for x in chips))
+        call([(mask3(k, m), sem["fin%d" % (m * NST // NSLAB)], [T.b[i] for i in range(len(chips))],
                [(c, T.b[m]) for c in col[k]])])
 
     if core == root:
@@ -190,16 +237,14 @@ def rank_program(g, core, T, topo):
 
     if in2:
         k = topo.chip(core)
-        used = [0, 0]
-        for p in range(NCALL):
+        per = NSLAB // NST
+        for p in range(NST):
             q = queues[p % 2]
-            q.wait_ge(sem["fin%d" % p], sum(_n(_common(topo, red[k][m], col[k])) for m in range(p * per, (p + 1) * per)))
+            q.wait_ge(sem["fin%d" % p], sum(_n(mask3(k, m)) for m in range(p * per, (p + 1) * per)))
             q.dma_start(T.y2[p * per * ROWS:(p + 1) * per * ROWS, :], T.b[p * per:(p + 1) * per]).then_inc(
                 sem["stq%d" % (p % 2)], 16)
-            used[p % 2] += 16
         for i in range(2):
-            if used[i]:
-                queues[i].wait_ge(sem["stq%d" % i], used[i])
+            queues[i].wait_ge(sem["stq%d" % i], 16 * len([p for p in range(NST) if p % 2 == i]))
     if in3:
         g.sync.wait_ge(sem.b3, _n(topo.mask(P["prev"][core], core)))
         g.sync.dma_start(T.y3[:], T.l3[:]).then_inc(sem.st3, 16)

@@ -2,18 +2,19 @@ from concourse.bass import DstId, RemoteDMATransfer
 
 WORLD = 512
 NSLAB = 4
-NST = 2
-ROWS = 128 // NSLAB
+NCH = 2
+NP = NSLAB * NCH
+ROWS = 128 // NP
 
 SCRATCH = {
-    "a": ("dram", [NSLAB, 128, 128], "float32"),
-    "b": ("dram", [NSLAB, 128, 128], "float32"),
+    "a": ("dram", [NP, 128, 512 // NP], "float32"),
+    "b": ("dram", [NP, 128, 512 // NP], "float32"),
     "c1": ("dram", [128, 16], "float32"),
     "s3": ("dram", [128, 8], "bfloat16"),
     "l3": ("dram", [128, 8], "bfloat16"),
 }
-SEMAPHORES = (["sent", "s0", "s1", "s2", "b1", "b3", "ldb", "ldx", "gst", "sty", "st3", "stq0", "stq1", "lda", "ldd"]
-              + ["fin%d" % p for p in range(NST)])
+SEMAPHORES = (["sent", "b1", "b3", "ldb", "ldx", "gst", "sty", "st3", "stq0", "stq1"]
+              + [n % p for p in range(NCH) for n in ("ld%d", "fin%d", "s0_%d", "s1_%d", "s2_%d")])
 
 _PLAN = {}
 
@@ -171,14 +172,10 @@ def rank_program(g, core, T, topo):
     in1 = core in P["g1"]
     root = P["root"]
 
-    def x2rows(lo, hi):
-        return T.x2[lo * ROWS:hi * ROWS, :]
-
     if in2:
-        fw, own, masks = _hop1_masks(topo, P, core)
-        if fw:
-            g.sync.dma_start(T.a[fw[0]:fw[-1] + 1], x2rows(fw[0], fw[-1] + 1)).then_inc(sem.lda, 16)
-        g.scalar.dma_start(T.a[own[0]:own[-1] + 1], x2rows(own[0], own[-1] + 1)).then_inc(sem.ldd, 16)
+        for p in range(NCH):
+            queues[p % 2].dma_start(T.a[p * NSLAB:(p + 1) * NSLAB], T.x2[p * NSLAB * ROWS:(p + 1) * NSLAB * ROWS, :]).then_inc(
+                sem["ld%d" % p], 16)
     if core == root:
         g.sync.dma_start(T.c1[:], T.x1[:]).then_inc(sem.ldb, 16)
         g.scalar.dma_start(T.y1[:], T.x1[:]).then_inc(sem.sty, 16)
@@ -188,35 +185,43 @@ def rank_program(g, core, T, topo):
     if in2:
         k = topo.chip(core)
         hi = col[k].index(core)
-        if fw:
-            g.wait_ge(sem.lda, 16)
-            call([(masks[m][0], sem.s0, [T.a[m]], [(snd[core][m], T.a[m])]) for m in fw])
-        g.wait_ge(sem.ldd, 16)
-        call([(masks[m][1], sem.s1, [T.a[m]], [(red[k][m], T.a[hi])]) for m in own])
+        nh = len(col[k])
+        fw, own, masks = _hop1_masks(topo, P, core)
+        for p in range(NCH):
+            g.wait_ge(sem["ld%d" % p], 16)
+            if fw:
+                call([(masks[m][0], sem["s0_%d" % p], [T.a[p * NSLAB + m]], [(snd[core][m], T.a[p * NSLAB + m])]) for m in fw])
+            call([(masks[m][1], sem["s1_%d" % p], [T.a[p * NSLAB + m]], [(red[k][m], T.a[p * nh + hi])]) for m in own])
 
     if core in P["fwdrole"]:
         c, m = P["fwdrole"][core]
         k = topo.chip(c)
         mk = _hop1_masks(topo, P, c)[2][m]
-        g.wait_ge(sem.s0, _n(mk[0]))
-        call([(mk[1], sem.s1, [T.a[m]], [(red[k][m], T.a[col[k].index(c)])])])
+        for p in range(NCH):
+            g.wait_ge(sem["s0_%d" % p], _n(mk[0]))
+            call([(mk[1], sem["s1_%d" % p], [T.a[p * NSLAB + m]], [(red[k][m], T.a[p * len(col[k]) + col[k].index(c)])])])
 
     def mask2(x, m):
         return _common(topo, red[x][m], [fin[y][m] for y in chips])
 
+    nc = len(chips)
     if core in P["redrole"]:
         k, m = P["redrole"][core]
-        g.wait_ge(sem.s1, sum(_n(_hop1_masks(topo, P, c)[2][m][1]) for c in col[k]))
-        call([(mask2(k, m), sem.s2, [T.a[i] for i in range(len(col[k]))], [(fin[y][m], T.b[chips.index(k)]) for y in chips])])
+        nh = len(col[k])
+        for p in range(NCH):
+            g.wait_ge(sem["s1_%d" % p], sum(_n(_hop1_masks(topo, P, c)[2][m][1]) for c in col[k]))
+            call([(mask2(k, m), sem["s2_%d" % p], [T.a[p * nh + i] for i in range(nh)],
+                   [(fin[y][m], T.b[p * nc + chips.index(k)]) for y in chips])])
 
     def mask3(k, m):
         return _common(topo, fin[k][m], col[k])
 
     if core in P["finrole"]:
         k, m = P["finrole"][core]
-        g.wait_ge(sem.s2, sum(_n(mask2(x, m)) for x in chips))
-        call([(mask3(k, m), sem["fin%d" % (m * NST // NSLAB)], [T.b[i] for i in range(len(chips))],
-               [(c, T.b[m]) for c in col[k]])])
+        for p in range(NCH):
+            g.wait_ge(sem["s2_%d" % p], sum(_n(mask2(x, m)) for x in chips))
+            call([(mask3(k, m), sem["fin%d" % p], [T.b[p * nc + i] for i in range(nc)],
+                   [(c, T.b[p * NSLAB + m]) for c in col[k]])])
 
     if core == root:
         g.wait_ge(sem.ldb, 16)
@@ -237,14 +242,15 @@ def rank_program(g, core, T, topo):
 
     if in2:
         k = topo.chip(core)
-        per = NSLAB // NST
-        for p in range(NST):
+        for p in range(NCH):
             q = queues[p % 2]
-            q.wait_ge(sem["fin%d" % p], sum(_n(mask3(k, m)) for m in range(p * per, (p + 1) * per)))
-            q.dma_start(T.y2[p * per * ROWS:(p + 1) * per * ROWS, :], T.b[p * per:(p + 1) * per]).then_inc(
+            q.wait_ge(sem["fin%d" % p], sum(_n(mask3(k, m)) for m in range(NSLAB)))
+            q.dma_start(T.y2[p * NSLAB * ROWS:(p + 1) * NSLAB * ROWS, :], T.b[p * NSLAB:(p + 1) * NSLAB]).then_inc(
                 sem["stq%d" % (p % 2)], 16)
         for i in range(2):
-            queues[i].wait_ge(sem["stq%d" % i], 16 * len([p for p in range(NST) if p % 2 == i]))
+            n = len([p for p in range(NCH) if p % 2 == i])
+            if n:
+                queues[i].wait_ge(sem["stq%d" % i], 16 * n)
     if in3:
         g.sync.wait_ge(sem.b3, _n(topo.mask(P["prev"][core], core)))
         g.sync.dma_start(T.y3[:], T.l3[:]).then_inc(sem.st3, 16)

@@ -2,7 +2,8 @@ from concourse.bass import DstId, RemoteDMATransfer
 
 WORLD = 512
 NSLAB = 4
-NCH = 2
+NCH = 4
+LAG = 2
 NP = NSLAB * NCH
 ROWS = 128 // NP
 
@@ -88,6 +89,7 @@ def _plan(T, topo):
         for c in col[k]:
             snd[c] = [c] * NSLAB if c == hubrank else lanes(c, True, red[k])
     P["mem"], P["col"], P["red"], P["fin"], P["snd"] = mem, col, red, fin, snd
+    P["chipmate"] = {c: [d for d in chip_cores(c) if d != c][:1] for c in mem}
     P["redrole"] = {red[k][m]: (k, m) for k in red for m in range(NSLAB)}
     P["finrole"] = {fin[k][m]: (k, m) for k in fin for m in range(NSLAB)}
     P["fwdrole"] = {snd[c][m]: (c, m) for c in snd for m in range(NSLAB) if snd[c][m] != c}
@@ -136,14 +138,14 @@ def _hop1_masks(topo, P, c):
     snd, red = P["snd"][c], P["red"][k]
     fw = [m for m in range(NSLAB) if snd[m] != c]
     own = [m for m in range(NSLAB) if snd[m] == c]
+    parts = _split(_common(topo, c, [snd[m] for m in fw] + [d for d in P["chipmate"][c]]), NSLAB)
     out = {}
-    if fw:
-        parts = _split(_common(topo, c, [snd[m] for m in fw]), NSLAB)[::-1]
-        for i, m in enumerate(fw):
-            out[m] = (parts[i], topo.mask(snd[m], red[m]))
-    parts = _split(_common(topo, c, [red[m] for m in own]), len(own))
-    for i, m in enumerate(own):
-        out[m] = (None, parts[i])
+    for m in own:
+        q = [x for x in parts if x & ~topo.mask(c, red[m]) == 0][0]
+        parts.remove(q)
+        out[m] = (None, q)
+    for m in fw:
+        out[m] = (parts.pop(), topo.mask(snd[m], red[m]))
     return fw, own, out
 
 
@@ -189,9 +191,8 @@ def rank_program(g, core, T, topo):
         fw, own, masks = _hop1_masks(topo, P, core)
         for p in range(NCH):
             g.wait_ge(sem["ld%d" % p], 16)
-            if fw:
-                call([(masks[m][0], sem["s0_%d" % p], [T.a[p * NSLAB + m]], [(snd[core][m], T.a[p * NSLAB + m])]) for m in fw])
-            call([(masks[m][1], sem["s1_%d" % p], [T.a[p * NSLAB + m]], [(red[k][m], T.a[p * nh + hi])]) for m in own])
+            call([(masks[m][0], sem["s0_%d" % p], [T.a[p * NSLAB + m]], [(snd[core][m], T.a[p * NSLAB + m])]) for m in fw]
+                 + [(masks[m][1], sem["s1_%d" % p], [T.a[p * NSLAB + m]], [(red[k][m], T.a[p * nh + hi])]) for m in own])
 
     if core in P["fwdrole"]:
         c, m = P["fwdrole"][core]
@@ -204,24 +205,29 @@ def rank_program(g, core, T, topo):
     def mask2(x, m):
         return _common(topo, red[x][m], [fin[y][m] for y in chips])
 
-    nc = len(chips)
-    if core in P["redrole"]:
-        k, m = P["redrole"][core]
-        nh = len(col[k])
-        for p in range(NCH):
-            g.wait_ge(sem["s1_%d" % p], sum(_n(_hop1_masks(topo, P, c)[2][m][1]) for c in col[k]))
-            call([(mask2(k, m), sem["s2_%d" % p], [T.a[p * nh + i] for i in range(nh)],
-                   [(fin[y][m], T.b[p * nc + chips.index(k)]) for y in chips])])
-
     def mask3(k, m):
         return _common(topo, fin[k][m], col[k])
 
-    if core in P["finrole"]:
+    nc = len(chips)
+
+    def reduce_chunk(p):
+        k, m = P["redrole"][core]
+        nh = len(col[k])
+        g.wait_ge(sem["s1_%d" % p], sum(_n(_hop1_masks(topo, P, c)[2][m][1]) for c in col[k]))
+        call([(mask2(k, m), sem["s2_%d" % p], [T.a[p * nh + i] for i in range(nh)],
+               [(fin[y][m], T.b[p * nc + chips.index(k)]) for y in chips])])
+
+    def finish_chunk(p):
         k, m = P["finrole"][core]
-        for p in range(NCH):
-            g.wait_ge(sem["s2_%d" % p], sum(_n(mask2(x, m)) for x in chips))
-            call([(mask3(k, m), sem["fin%d" % p], [T.b[p * nc + i] for i in range(nc)],
-                   [(c, T.b[p * NSLAB + m]) for c in col[k]])])
+        g.wait_ge(sem["s2_%d" % p], sum(_n(mask2(x, m)) for x in chips))
+        call([(mask3(k, m), sem["fin%d" % p], [T.b[p * nc + i] for i in range(nc)],
+               [(c, T.b[p * NSLAB + m]) for c in col[k]])])
+
+    for i in range(NCH + LAG):
+        if core in P["redrole"] and i < NCH:
+            reduce_chunk(i)
+        if core in P["finrole"] and i >= LAG:
+            finish_chunk(i - LAG)
 
     if core == root:
         g.wait_ge(sem.ldb, 16)

@@ -37,6 +37,16 @@ def _common(topo, src, dsts):
     return m
 
 
+def _groups(topo, src, dsts):
+    low = _common(topo, src, dsts)
+    narrow = [d for d in dsts if not topo.mask(src, d) & ~low]
+    out = {d: q for d, q in zip(narrow, _split(low, len(narrow)))}
+    for d in dsts:
+        if d not in out:
+            out[d] = topo.mask(src, d) & ~low
+    return out
+
+
 def _plan(T, topo):
     if "p" in _PLAN:
         return _PLAN["p"]
@@ -203,25 +213,26 @@ def rank_program(g, core, T, topo):
             call([(mk[1], sem["s1_%d" % p], [T.a[p * NSLAB + m]], [(red[k][m], T.a[p * len(col[k]) + col[k].index(c)])])])
 
     def mask2(x, m):
-        return _common(topo, red[x][m], [fin[y][m] for y in chips])
+        return _groups(topo, red[x][m], [fin[y][m] for y in chips])
 
     def mask3(k, m):
-        return _common(topo, fin[k][m], col[k])
+        return _groups(topo, fin[k][m], col[k])
 
     nc = len(chips)
 
     def reduce_chunk(p):
         k, m = P["redrole"][core]
         nh = len(col[k])
+        mk = mask2(k, m)
         g.wait_ge(sem["s1_%d" % p], sum(_n(_hop1_masks(topo, P, c)[2][m][1]) for c in col[k]))
-        call([(mask2(k, m), sem["s2_%d" % p], [T.a[p * nh + i] for i in range(nh)],
-               [(fin[y][m], T.b[p * nc + chips.index(k)]) for y in chips])])
+        call([(mk[fin[y][m]], sem["s2_%d" % p], [T.a[p * nh + i] for i in range(nh)],
+               [(fin[y][m], T.b[p * nc + chips.index(k)])]) for y in chips])
 
     def finish_chunk(p):
         k, m = P["finrole"][core]
-        g.wait_ge(sem["s2_%d" % p], sum(_n(mask2(x, m)) for x in chips))
-        call([(mask3(k, m), sem["fin%d" % p], [T.b[p * nc + i] for i in range(nc)],
-               [(c, T.b[p * NSLAB + m]) for c in col[k]])])
+        mk = mask3(k, m)
+        g.wait_ge(sem["s2_%d" % p], sum(_n(mask2(x, m)[core]) for x in chips))
+        call([(mk[c], sem["fin%d" % p], [T.b[p * nc + i] for i in range(nc)], [(c, T.b[p * NSLAB + m])]) for c in col[k]])
 
     for i in range(NCH + LAG):
         if core in P["redrole"] and i < NCH:
@@ -250,7 +261,7 @@ def rank_program(g, core, T, topo):
         k = topo.chip(core)
         for p in range(NCH):
             q = queues[p % 2]
-            q.wait_ge(sem["fin%d" % p], sum(_n(mask3(k, m)) for m in range(NSLAB)))
+            q.wait_ge(sem["fin%d" % p], sum(_n(mask3(k, m)[core]) for m in range(NSLAB)))
             q.dma_start(T.y2[p * NSLAB * ROWS:(p + 1) * NSLAB * ROWS, :], T.b[p * NSLAB:(p + 1) * NSLAB]).then_inc(
                 sem["stq%d" % (p % 2)], 16)
         for i in range(2):

from concourse.bass import DstId, RemoteDMATransfer

WORLD = 512
NSLAB = 4
NCH = 4
LAG = 2
NP = NSLAB * NCH
ROWS = 128 // NP

SCRATCH = {
    "a": ("dram", [NP, 128, 512 // NP], "float32"),
    "b": ("dram", [NP, 128, 512 // NP], "float32"),
    "c1": ("dram", [128, 16], "float32"),
    "s3": ("dram", [128, 8], "bfloat16"),
    "l3": ("dram", [128, 8], "bfloat16"),
}
SEMAPHORES = (["sent", "b1", "b3", "ldb", "ldx", "gst", "sty", "st3", "stq0", "stq1"]
              + [n % p for p in range(NCH) for n in ("ld%d", "fin%d", "s0_%d", "s1_%d", "s2_%d")])

_PLAN = {}


def _n(mask):
    return bin(mask).count("1")


def _split(mask, n):
    bits = [i for i in range(mask.bit_length()) if (mask >> i) & 1]
    w = len(bits) // n
    return [sum(1 << e for e in bits[i * w:(i + 1) * w]) for i in range(n)]


def _common(topo, src, dsts):
    m = topo.mask(src, dsts[0])
    for d in dsts[1:]:
        m &= topo.mask(src, d)
    return m


def _groups(topo, src, dsts):
    low = _common(topo, src, dsts)
    narrow = [d for d in dsts if not topo.mask(src, d) & ~low]
    out = {d: q for d, q in zip(narrow, _split(low, len(narrow)))}
    for d in dsts:
        if d not in out:
            out[d] = topo.mask(src, d) & ~low
    return out


def _plan(T, topo):
    if "p" in _PLAN:
        return _PLAN["p"]
    cores = list(T.cores)
    tb = T.tables
    world = range(WORLD)

    def chip_cores(c):
        return [d for d in world if topo.host(d) == topo.host(c) and topo.chip(d) == topo.chip(c)]

    def owns_port(d):
        return topo.may_write(d, [e for e in world if topo.mates(d, e)][0])

    def port_cores(c):
        own = [d for d in chip_cores(c) if d not in cores and owns_port(d)]
        dies = sorted({topo.die(d) for d in own}, key=lambda x: x == topo.die(c))
        by = [[d for d in own if topo.die(d) == x] for x in dies]
        return [by[i % len(by)][i // len(by)] for i in range(len(own))]

    def lanes(c, with_rank, reds):
        out = [None] * len(reds)
        for die in sorted({topo.die(r) for r in reds}):
            slabs = [m for m in range(len(reds)) if topo.die(reds[m]) == die]
            pick = []
            for port in (True, False):
                cl = [d for d in chip_cores(c) if topo.die(d) == die and owns_port(d) == port]
                if c in cl:
                    cl = [c] if with_rank else [d for d in cl if d != c]
                pick.append(cl[0])
            for m, d in zip(slabs, pick if with_rank else pick[::-1]):
                out[m] = d
        return out

    P = {}
    mem = [cores[r] for r in tb["G2"]]
    hosts = sorted({topo.host(c) for c in mem})
    col = {}
    for c in mem:
        col.setdefault(topo.chip(c), []).append(c)
    for k in col:
        col[k].sort(key=topo.host)
    hub = [h for h in hosts
           if all(topo.may_write(c, d) and topo.may_write(d, c)
                  for k in col for c in col[k] for d in col[k] if topo.host(d) == h and c != d)][0]
    red, fin, snd = {}, {}, {}
    for k in col:
        hubrank = [c for c in col[k] if topo.host(c) == hub][0]
        red[k] = port_cores(hubrank)[:NSLAB]
        fin[k] = lanes(hubrank, False, red[k])
        for c in col[k]:
            snd[c] = [c] * NSLAB if c == hubrank else lanes(c, True, red[k])
    P["mem"], P["col"], P["red"], P["fin"], P["snd"] = mem, col, red, fin, snd
    P["chipmate"] = {c: [d for d in chip_cores(c) if d != c][:1] for c in mem}
    P["redrole"] = {red[k][m]: (k, m) for k in red for m in range(NSLAB)}
    P["finrole"] = {fin[k][m]: (k, m) for k in fin for m in range(NSLAB)}
    P["fwdrole"] = {snd[c][m]: (c, m) for c in snd for m in range(NSLAB) if snd[c][m] != c}
    busy = set(cores) | set(P["redrole"]) | set(P["finrole"]) | set(P["fwdrole"])

    g1 = [cores[r] for r in tb["G1"]]
    root = g1[tb["ROOT1"]]
    dests = [d for d in g1 if d != root]
    direct = [d for d in dests if topo.may_write(root, d)]
    rest = [d for d in dests if d not in direct]
    relays = {}
    for rk in sorted({topo.rack(topo.host(d)) for d in rest}):
        ds = [d for d in rest if topo.rack(topo.host(d)) == rk]
        cands = [c for c in world if c not in busy and topo.rack(topo.host(c)) == rk and topo.chip(c) == topo.chip(root)
                 and topo.may_write(root, c) and all(topo.may_write(c, d) for d in ds)]
        cands.sort(key=lambda c: (topo.host(c) != topo.host(root), topo.die(c) != topo.die(root)))
        relays[cands[0]] = ds
        busy.add(cands[0])
    P["root"], P["direct"], P["relays"], P["g1"] = root, direct, relays, g1
    from1 = {d: root for d in direct + list(relays)}
    for c in relays:
        for d in relays[c]:
            from1[d] = c
    P["mask1"] = {root: _common(topo, root, direct + list(relays))}
    for c in relays:
        P["mask1"][c] = _common(topo, c, relays[c])
    P["from1"] = from1

    g3 = [cores[r] for r in tb["G3"]]
    nxt, prev = {}, {}
    for i, s in enumerate(g3):
        d = g3[(i + 1) % len(g3)]
        if topo.may_write(s, d):
            nxt[s], prev[d] = d, s
        else:
            rl = [c for c in port_cores(s) if c not in busy and topo.may_write(c, d)][0]
            busy.add(rl)
            nxt[s], prev[rl], nxt[rl], prev[d] = rl, s, d, rl
    P["g3"], P["nxt"], P["prev"] = g3, nxt, prev
    _PLAN["p"] = P
    return P


def _hop1_masks(topo, P, c):
    k = topo.chip(c)
    snd, red = P["snd"][c], P["red"][k]
    fw = [m for m in range(NSLAB) if snd[m] != c]
    own = [m for m in range(NSLAB) if snd[m] == c]
    parts = _split(_common(topo, c, [snd[m] for m in fw] + [d for d in P["chipmate"][c]]), NSLAB)
    out = {}
    for m in own:
        q = [x for x in parts if x & ~topo.mask(c, red[m]) == 0][0]
        parts.remove(q)
        out[m] = (None, q)
    for m in fw:
        out[m] = (parts.pop(), topo.mask(snd[m], red[m]))
    return fw, own, out


def rank_program(g, core, T, topo):
    P = _plan(T, topo)
    sem = T.sem
    sent = [0]

    def dst(d):
        rid, pid = topo.addr(d, core)
        return DstId(rid=rid, pnc=pid)

    def call(specs):
        trs = []
        for mask, rsem, srcs, outs in specs:
            trs.append(RemoteDMATransfer(dst_ids=[dst(d) for d, _ in outs], dma_engine_mask=mask, remote_sem=rsem,
                                         srcs=list(srcs), dsts=[ap for _, ap in outs], alu_op=1 if len(srcs) > 1 else 0))
            sent[0] += _n(mask)
        g.remote_dma_fused(trs, local_sem=sem.sent)

    mem, col, red, fin, snd = P["mem"], P["col"], P["red"], P["fin"], P["snd"]
    chips = sorted(col)
    queues = (g.sync, g.scalar)
    in2 = core in mem
    in3 = core in P["g3"]
    in1 = core in P["g1"]
    root = P["root"]

    if in2:
        for p in range(NCH):
            queues[p % 2].dma_start(T.a[p * NSLAB:(p + 1) * NSLAB], T.x2[p * NSLAB * ROWS:(p + 1) * NSLAB * ROWS, :]).then_inc(
                sem["ld%d" % p], 16)
    if core == root:
        g.sync.dma_start(T.c1[:], T.x1[:]).then_inc(sem.ldb, 16)
        g.scalar.dma_start(T.y1[:], T.x1[:]).then_inc(sem.sty, 16)
    if in3:
        g.sync.dma_start(T.s3[:], T.x3[:]).then_inc(sem.ldx, 16)

    if in2:
        k = topo.chip(core)
        hi = col[k].index(core)
        nh = len(col[k])
        fw, own, masks = _hop1_masks(topo, P, core)
        for p in range(NCH):
            g.wait_ge(sem["ld%d" % p], 16)
            call([(masks[m][0], sem["s0_%d" % p], [T.a[p * NSLAB + m]], [(snd[core][m], T.a[p * NSLAB + m])]) for m in fw]
                 + [(masks[m][1], sem["s1_%d" % p], [T.a[p * NSLAB + m]], [(red[k][m], T.a[p * nh + hi])]) for m in own])

    if core in P["fwdrole"]:
        c, m = P["fwdrole"][core]
        k = topo.chip(c)
        mk = _hop1_masks(topo, P, c)[2][m]
        for p in range(NCH):
            g.wait_ge(sem["s0_%d" % p], _n(mk[0]))
            call([(mk[1], sem["s1_%d" % p], [T.a[p * NSLAB + m]], [(red[k][m], T.a[p * len(col[k]) + col[k].index(c)])])])

    def mask2(x, m):
        return _groups(topo, red[x][m], [fin[y][m] for y in chips])

    def mask3(k, m):
        return _groups(topo, fin[k][m], col[k])

    nc = len(chips)

    def reduce_chunk(p):
        k, m = P["redrole"][core]
        nh = len(col[k])
        mk = mask2(k, m)
        g.wait_ge(sem["s1_%d" % p], sum(_n(_hop1_masks(topo, P, c)[2][m][1]) for c in col[k]))
        call([(mk[fin[y][m]], sem["s2_%d" % p], [T.a[p * nh + i] for i in range(nh)],
               [(fin[y][m], T.b[p * nc + chips.index(k)])]) for y in chips])

    def finish_chunk(p):
        k, m = P["finrole"][core]
        mk = mask3(k, m)
        g.wait_ge(sem["s2_%d" % p], sum(_n(mask2(x, m)[core]) for x in chips))
        call([(mk[c], sem["fin%d" % p], [T.b[p * nc + i] for i in range(nc)], [(c, T.b[p * NSLAB + m])]) for c in col[k]])

    for i in range(NCH + LAG):
        if core in P["redrole"] and i < NCH:
            reduce_chunk(i)
        if core in P["finrole"] and i >= LAG:
            finish_chunk(i - LAG)

    if core == root:
        g.wait_ge(sem.ldb, 16)
        call([(P["mask1"][root], sem.b1, [T.c1[:]], [(d, T.c1[:]) for d in P["direct"] + list(P["relays"])])])
    if core in P["relays"]:
        g.wait_ge(sem.b1, _n(P["mask1"][root]))
        call([(P["mask1"][core], sem.b1, [T.c1[:]], [(d, T.c1[:]) for d in P["relays"][core]])])

    if core in P["nxt"]:
        d = P["nxt"][core]
        if in3:
            g.wait_ge(sem.ldx, 16)
            src = T.s3[:]
        else:
            g.wait_ge(sem.b3, _n(topo.mask(P["prev"][core], core)))
            src = T.l3[:]
        call([(topo.mask(core, d), sem.b3, [src], [(d, T.l3[:])])])

    if in2:
        k = topo.chip(core)
        for p in range(NCH):
            q = queues[p % 2]
            q.wait_ge(sem["fin%d" % p], sum(_n(mask3(k, m)[core]) for m in range(NSLAB)))
            q.dma_start(T.y2[p * NSLAB * ROWS:(p + 1) * NSLAB * ROWS, :], T.b[p * NSLAB:(p + 1) * NSLAB]).then_inc(
                sem["stq%d" % (p % 2)], 16)
        for i in range(2):
            n = len([p for p in range(NCH) if p % 2 == i])
            if n:
                queues[i].wait_ge(sem["stq%d" % i], 16 * n)
    if in3:
        g.sync.wait_ge(sem.b3, _n(topo.mask(P["prev"][core], core)))
        g.sync.dma_start(T.y3[:], T.l3[:]).then_inc(sem.st3, 16)
        g.sync.wait_ge(sem.st3, 16)
    if core == root:
        g.scalar.wait_ge(sem.sty, 16)
    elif in1:
        n1 = _n(P["mask1"][P["from1"][core]])
        if in2:
            g.wait_ge(sem.b1, n1)
            g.dma_start(T.y1[:], T.c1[:]).then_inc(sem.gst, 16)
            g.wait_ge(sem.gst, 16)
        else:
            g.scalar.wait_ge(sem.b1, n1)
            g.scalar.dma_start(T.y1[:], T.c1[:]).then_inc(sem.sty, 16)
            g.scalar.wait_ge(sem.sty, 16)
    if sent[0]:
        g.wait_ge(sem.sent, sent[0])
